import numpy as np, ml_dtypes
CORES = [10,34,74,98]
N = 4
BF = ml_dtypes.bfloat16
V, U, H, S, Q, P, ST, RO, NEED = 2816, 1024, 256, 128, 2, 256, 128, 5, 9
def noisy(rng, base, part):
    return base[:, :, None, :] * (1 + part * (2 * rng.random((N, 8, 16, V)) - 1))
def detours(rng, m, share):
    hub = rng.integers(0, V, (N, 8, m)); h = np.take_along_axis(hub, rng.integers(0, m, (N, 8, 16 * U)), 2).reshape(N, 8, 16, U)
    p = np.where(rng.random((N, 8, 16, U)) < share, h, rng.integers(0, V, (N, 8, 16, U)))
    return p, rng.integers(0, V, (N, 8, 16, U))
def pack(x, p, q):
    x = x.astype(np.float32); x[..., V - H:] = np.roll(x, -1, axis=0)[..., :H]
    e = np.arange(U); p = np.where(p == e, (p + 1) % V, p)
    for i in range(2): q = np.where((q == e) | (q == p), (q + 1) % V, q)
    return {"dist": np.ascontiguousarray(x.reshape(N, 128, V)), "b1": np.ascontiguousarray(p.reshape(N, 128, U)).astype(np.int32), "b2": np.ascontiguousarray(q.reshape(N, 128, U)).astype(np.int32)}
def plain(rng):
    hot = rng.permuted(np.tile(np.array([0.03, 0.05, 0.07, 0.09, 0.12, 0.16, 0.25, 0.4]), (N, 1)), axis=1)[..., None]
    u, w = rng.random((N, 8, V)), rng.random((N, 8, V)); base = 0.8 + 0.4 * rng.random((N, 8, V))
    base = np.where(u < hot, 2 + 2.5 * w * w, np.where(u > 0.97, 0.25 + 0.25 * w, base))
    p, q = detours(rng, 24, 0.5)
    return noisy(rng, base, 0.15), p, q
def quiet(rng, n):
    x = 1 + 0.03 * (2 * rng.random((N, 16, V)) - 1); mid = U + np.argsort(rng.random((N, V - H - U)), axis=1); h = (V - H - U - n) // 2
    p = np.take_along_axis(mid[:, n:n + h], rng.integers(0, h, (N, 16 * U)), 1).reshape(N, 16, U)
    q = np.take_along_axis(mid[:, n + h:n + 2 * h], rng.integers(0, h, (N, 16 * U)), 1).reshape(N, 16, U)
    return x, p, q, mid[:, :n]
def ties(rng, size):
    n = 32; x, p, q, o = quiet(rng, 2 * n); kind = np.arange(n) % 4
    for r in range(N):
        e = rng.permutation(U)[:n]; one, two = o[r, :n], o[r, n:]
        m = rng.integers(192, 256, (16, n)) * 2 ** 16 + rng.integers(2 ** 10, 2 ** 15 - 2 ** 10, (16, n)) + 2 ** 15 * (kind == 3)
        j = rng.integers(2 ** 21, 2 ** 22, (16, n)); up = np.argsort(rng.random((16, n)), axis=0) < np.array([0, 8, 9, 16])[kind]
        x[r][:, e] = (m + up) * 2.0 ** -23; x[r][:, one] = (m - j - 1) * 2.0 ** -23; x[r][:, two] = (4 * j + 3) * 2.0 ** -25
        p[r][:, e] = one; q[r][:, e] = two
    return x * size, p, q
def still(rng):
    x, p, q, o = quiet(rng, Q + 3); f = 1 + 0.05 * rng.random((16, 1)); turn = int(rng.integers(0, 2))
    for r in range(N):
        if r % 2 != turn: continue
        i = rng.permutation(H)[:2 * Q]; a, b = np.sort(i[:Q]), i[Q:]
        x[r][:, a] = 10 * f; x[r][:, b] = f; x[r][:, o[r, :Q]] = f; p[r][:, a] = b; q[r][:, a] = o[r, :Q]
        x[r][:, o[r, Q:Q + 2]] = 8.0; p[r][:, b] = o[r, Q]; q[r][:, b] = o[r, Q + 1]
        s = (r - 1) % N; m = rng.random(U) < 0.05; m[:P * (RO - 1 - Q)] = False; m[ST * (RO - 1) % U] = True; m[U - 1] = True; e = np.nonzero(m)[0]
        x[s][:, e] = 5 * f; x[s, :, o[s, Q + 2]] = f[:, 0]; p[s][:, e] = V - H + b[(RO - 2) % Q]; q[s][:, e] = o[s, Q + 2]
    return x, p, q
def below(rng):
    n = 20; w = 2 * Q; k = 5 + 2 * (w - 3); x, p, q, o = quiet(rng, n * k); odd = np.arange(16) % 2
    for r in range(N):
        f = 1 + 0.05 * rng.random(16); e = np.sort(rng.permutation(ST)[:n * w]).reshape(n, w); spare = rng.permutation(n); d = o[r].reshape(n, k)
        for i in range(n):
            a, b, far = e[i, 0], e[i, 1], e[i, Q + 1]; c, y1, y2, w1, v = d[i, :5]; late = U - 1 - i
            for edge, size in ((a, 8.0), (b, 1.0), (far, 100.0), (c, 1.0), (y1, 0.25), (y2, 0.25), (w1, 1.0), (v, 8.4), (late, 8.0)): x[r, :, edge] = size * f
            if spare[i] < 16: x[r, spare[i], far] = 1.5 * f[spare[i]]
            p[r, :, a] = b; q[r, :, a] = np.where(odd == 1, v, c); p[r, :, b] = y1; q[r, :, b] = y2
            p[r, :, far] = c; q[r, :, far] = w1; p[r, :, late] = b; q[r, :, late] = v
            for j, edge in enumerate(np.delete(e[i], [0, 1, Q + 1])):
                x[r, :, edge] = 4 * f; p[r, :, edge] = d[i, 5 + 2 * j]; q[r, :, edge] = d[i, 6 + 2 * j]
    return x, p, q
def setup_inputs(rng):
    x, p, q = plain(rng)
    return pack(x, p, q)
def setup_inputs_spread(rng):
    base = np.exp2(6 * rng.random((N, 8, V)) - 3) * (rng.random((N, 8, V)) > 0.03125)
    p, q = detours(rng, 48, 0.3); x = noisy(rng, base, 0.25); gs = rng.permutation(8)
    x[:, gs[0]] *= 64.0; x[:, gs[1]] *= 2.0 ** -24
    for g, size in ((gs[2], 512.0), (gs[3], 2.0 ** -22)):
        x[:, g], p[:, g], q[:, g] = ties(rng, size)
    return pack(x, p, q)
def setup_inputs_ends(rng):
    typ = (np.arange(N)[:, None] + np.arange(8)[None, :]) % 2
    base = np.where(rng.random((N, 8, V)) < 0.35, 8.0, 0.125); base[:, 7, :P] = 8.0; base[:, :, U - 1] = 8.0
    base[:, :, 0] = np.where(typ == 0, 8.0, 0.125); base[:, :, H - 1] = np.where(typ == 1, 8.0, 0.125)
    x = base[:, :, None, :] * (1 - 0.05 * rng.random((N, 8, 16, V)))
    p, q = detours(rng, 24, 0.1)
    m = np.argsort(rng.random((N, 8, 16, U)), axis=2) < 11; a = (V - 1) * rng.integers(0, 2, (N, 8, 16, U))
    return pack(x, np.where(m, a, p), np.where(m, V - 1 - a, q))
def setup_inputs_corners(rng):
    wall = V - H - 1; x = noisy(rng, 0.7 + 0.2 * rng.random((N, 8, V)), 0.05)
    hub = rng.integers(U, wall, (N, 8, 16)); h = np.take_along_axis(hub, rng.integers(0, 16, (N, 8, 16 * U)), 2).reshape(N, 8, 16, U)
    p = np.where(rng.random((N, 8, 16, U)) < 0.5, h, rng.integers(U, wall, (N, 8, 16, U))); q = rng.integers(U, wall, (N, 8, 16, U))
    p = np.where(np.arange(16)[:, None] < rng.integers(0, 16, (N, 8, 1, U)), wall, p)
    m = rng.random((N, 8, U)) < 0.1; m[..., :P] = False; rows = np.ones((N, 8, 16, U), bool); w = rng.random((N, 8, 1, U))
    long = (2.2 + 3 * w * w) * (1 + 0.05 * (2 * rng.random((N, 8, 16, U)) - 1)); pairs = np.arange(32)
    late = int(rng.integers(0, 8)); fr = min(RO - 2, (U - 1) // P); e = slice(P * fr, P * fr + 16 * Q)
    for r in range(N):
        order = rng.permutation(8); i = int(np.argmax(order == 5)); order[i] = order[late]; order[late] = 5
        for g in range(8):
            kind = order[g]
            if kind < 5: m[r, g, rng.permutation(P)[:(S - 1, S, S + 1, P, 1)[kind]]] = True
            elif kind == 5 and r % 2 == 0:
                flip = np.repeat(rng.integers(0, 2, 16), 2); m[r, g, :32] = True
                p[r, g, :, :32] = U + np.repeat(rng.permutation(wall - U)[:16], 2)
                long[r, g, :, :32] = np.where(pairs % 2 == flip, 6.0, 2.2) * (1 + 0.05 * (2 * rng.random((16, 32)) - 1))
            elif kind == 5:
                m[r, g] = False; m[r, g, e] = True; o = U + rng.permutation(wall - U)[:16 + 16 * Q]
                c = o[16:].copy(); c[(RO - 1) % Q::Q] = V - H + 32 + rng.permutation(H - 32)[:16]
                p[r, g, :, e] = np.repeat(o[:16], Q); q[r, g, :, e] = c
                long[r, g, :, e] = np.where(np.arange(16 * Q) % Q == fr % Q, 6.0, 2.2) * (1 + 0.05 * (2 * rng.random((16, 16 * Q)) - 1))
            else:
                m[r, g, :P] = True; c = rng.choice(np.array([8, 9] if kind == 6 else [0, 9, 15, 16]), P)
                rows[r, g, :, :P] = np.argsort(rng.random((16, P)), axis=0) < c
    x[..., :U] = np.where(m[:, :, None, :] & rows, long, x[..., :U]); x[..., wall] = 8.0
    return pack(x, p, q)
def setup_inputs_calm(rng):
    x, p, q = plain(rng); og = rng.permutation(8); gs = og[:4]
    x[:, gs] = noisy(rng, 0.9 + 0.2 * rng.random((N, 8, V)), 0.05)[:, gs]
    for r in range(N):
        for i in range(4):
            c = np.concatenate([rng.permutation(ST)[:(i + r) % 4], U - 1 - rng.permutation(64)[:1]])
            x[r, gs[i], :, c] = 2.6 * (1 + 0.03 * (2 * rng.random((len(c), 16)) - 1))
    x[:, og[4]], p[:, og[4]], q[:, og[4]] = still(rng)
    x[:, og[5]], p[:, og[5]], q[:, og[5]] = below(rng)
    return pack(x, p, q)
def setup_inputs_crowd(rng):
    x = 0.25 * (rng.integers(4, 17, (N, 8, 1, V)) + rng.integers(0, 2, (N, 8, 16, V)))
    p, q = detours(rng, 24, 0.2)
    for r in range(N):
        for g in range(8):
            kind = (g + r) % 4; hs = U + rng.permutation(V - H - U)[:8]
            x[r, g, :, hs] = 0.25 * (1 + rng.integers(0, 2, (8, 16)))
            if kind < 2:
                e = rng.integers(0, P); a, b = p[r, g, :, e].copy(), q[r, g, :, e].copy()
                p[r, g] = hs[0]; q[r, g] = hs[1]
                if kind == 1: p[r, g, :, e] = a; q[r, g, :, e] = b
            elif kind == 2: p[r, g] = hs[0]
            else: p[r, g] = hs[rng.integers(0, 8, (16, U))]; q[r, g] = hs[rng.integers(0, 8, (16, U))]
    return pack(x, p, q)
def check_inputs(d):
    bad = []; x, p, q = np.asarray(d["dist"]), np.asarray(d["b1"]), np.asarray(d["b2"]); e = np.arange(U)
    if not np.all((x >= 0) & (x <= 1024)): bad.append("range of dist")
    if np.min(p) < 0 or np.max(p) > V - 1: bad.append("range of b1")
    if np.min(q) < 0 or np.max(q) > V - 1: bad.append("range of b2")
    if np.any((p == e) | (q == e) | (p == q)): bad.append("the three edges of a triple in b1 and b2 differ")
    if not np.array_equal(np.roll(x, -1, axis=0)[..., :H], x[..., V - H:]): bad.append("shared columns of dist")
    return bad
def reference(dist, b1, b2):
    D = dist.astype(np.float32).reshape(N, 8, 16, V); B1 = b1.astype(np.int64).reshape(N, 8, 16, U); B2 = b2.astype(np.int64).reshape(N, 8, 16, U)
    flag = np.ones((N, 8, U), bool); fill = np.zeros((N, 8, S), bool); tri = np.full((N, 8, 3, S), -1, np.int64); z = np.zeros((N, 8, 16, S), np.float32)
    for t in range(RO):
        corr = np.zeros((N, 8, 16, V), np.float32); touch = np.zeros((N, 8, V), bool); order = (ST * t + np.arange(U)) % U
        for r in range(N):
            for g in range(8):
                x = D[r, g]
                look = order[flag[r, g, order]][:P]; flag[r, g, look] = False
                c1, c2 = B1[r, g][:, look], B2[r, g][:, look]
                n = np.sum(x[:, look][:, None, :] > x[:, c1] + x[:, c2], axis=0)
                k = np.argmax(n, axis=0)
                who = np.nonzero(np.max(n, axis=0) >= NEED)[0]; free = np.nonzero(~fill[r, g])[0]
                m = min(len(who), len(free)); who, s = who[:m], free[:m]
                tri[r, g][0, s] = look[who]; tri[r, g][1, s] = c1[k[who], who]; tri[r, g][2, s] = c2[k[who], who]
                fill[r, g, s] = True; z[r, g][:, s] = 0
                vis = np.arange(t % Q, S, Q); vis = vis[fill[r, g, vis]]; w = tri[r, g][:, vis]
                least = np.full(V, S, np.int64); np.minimum.at(least, w, np.broadcast_to(vis, w.shape))
                st = vis[np.all(least[w] == vis, axis=0)]
                a, b, c = tri[r, g][:, st]; old = z[r, g][:, st]
                theta = ((x[:, a] - x[:, b]) - x[:, c]) * np.float32(0.5)
                delta = np.maximum(theta, -old); new = old + delta
                z[r, g][:, st] = new
                corr[r, g][:, a] = -delta; corr[r, g][:, b] = delta; corr[r, g][:, c] = delta
                touch[r, g, a] = True; touch[r, g, b] = True; touch[r, g, c] = True
                gone = st[np.all(new == 0, axis=0)]; fill[r, g, gone] = False; tri[r, g][:, gone] = -1
        nxt = D + corr
        for r in range(N):
            for q, mine, other in (((r - 1) % N, slice(0, H), slice(V - H, V)), ((r + 1) % N, slice(V - H, V), slice(0, H))):
                own, his = corr[r][..., mine], corr[q][..., other]
                one, two = (own, his) if r < q else (his, own)
                nxt[r][..., mine] = (D[r][..., mine] + one) + two
        D = nxt
        flag = flag | touch[..., :U]
        flag[:, :, :H] = flag[:, :, :H] | np.roll(touch, 1, axis=0)[..., V - H:]
    return {"yd": D.reshape(N, 128, V), "yz": z.reshape(N, 128, S), "yt": tri.reshape(N, 8, 3 * S).astype(np.float32), "yf": flag.astype(np.float32)}

import math
from concourse.bass import DstId, RemoteDMATransfer
from concourse.mybir import AluOpType as ALU, ActivationFunctionType as ACT

V, U, H, RO = 2816, 1024, 256, 5
CEN = 1408.0
YS = 128.0
RP, TB = 256, 520
RL = 1024
LN = math.log(3.0)
CFG = {"parts": [64, 128, 64], "chunks": [[16, 16, 16, 16], [32, 32, 32, 32], [32, 32]], "waw": True, "trans": True,
       "psadd": 32, "seq": True, "cut": 2, "rep": 4, "comb": True,
       "hold": True}

F32, B16, F16, I32, U16 = "float32", "bfloat16", "float16", "int32", "uint16"
SB = {
    "bw": (6848, F32), "b1s": (1032, I32), "b2s": (1032, I32), "o1": (256, U16), "o2": (256, U16),
    "s1": (4096, F32), "sm": (4096, F32), "cm": (4096, B16), "de": (256, F32), "wx": (256, B16), "oc": (512, B16),
    "p1": (256, F32), "p2": (256, F32), "rv": (256, F32), "cw": (648, F32), "lw": (2056, F32), "lh": (256, F16),
    "lu": (16, U16), "inv": (256, B16), "tw": (6848, B16), "ta": (16, F32), "tb": (16, F32), "pu": (16, U16),
    "gu": (8, U16), "th": (128, F16), "fr": (128, B16), "ys": (192, F32), "yu": (12, U16), "mu": (12, U16),
    "ab": (12, F32), "mm": (12, F32), "mo": (12, F32), "pre": (12, F32), "prt": (12, F32), "ou": (12, U16), "tu": (12, U16),
    "eq": (1440, B16), "dg": (192, F32), "bs": (192, F32), "t1": (64, F32), "t2": (64, F32), "d2": (64, F32),
    "dl": (192, F32), "nz2": (64, F32), "mk": (64, F32), "sw": (64, F32), "sr": (64, F32), "dm": (64, F32),
    "z": (128, F32), "nzb": (256, B16), "nsb": (256, B16), "fs": (256, B16), "g1": (8, F32), "g2": (8, F32), "g3": (8, F32),
    "ll": (1280, F32), "lr": (1280, F32), "ts": (80, F32), "tl": (80, F32), "thr": (64, F32), "fw": (64, B16),
    "fq": (272, B16), "f1": (64, F32), "sc": (68, F32), "of": (64, F32), "fu": (64, U16), "cn": (2, F32), "tq": (64, F32),
    "tf": (128, F32), "ft": (1024, F32),
    "ia": (128, F32), "colp": (192, F32), "pi": (2, I32), "cc": (24, F32), "k1": (128, F32), "k2": (128, F32), "k3": (128, F32),
    "s2": (1024, F32), "sq": (432, F32), "eqs": (432, B16),
    "bm": (128, B16), "idn": (128, B16), "um": (128, B16), "bu": (128, B16), "mz": (128, B16), "n64": (128, B16),
    "ee": (2048, B16), "e1f": (128, F32), "e2f": (128, F32), "ra": (128, B16), "rr": (384, B16), "nr0": (128, B16),
    "xm": (192, B16), "rst": (192, F32), "rm": (480, B16), "negm": (64, F32), "rs64": (64, F32), "nege": (1536, F32),
    "ew": (64, F32), "i1": (64, F32), "m16": (68, F32), "dk": (128, F32), "zr": (128, F32), "c16": (8, F32), "c256": (8, F32),
    "dmp": (12, F32), "dmt": (12, F32), "stp": (960, B16), "fre": (128, F32), "sel": (128, B16), "om": (24, F32), "tm": (24, F32),
}
SCRATCH = {n: ("sbuf", [128, w], d) for n, (w, d) in SB.items()}
SCRATCH.update({"ps%d" % i: ("psum", [128, 512], F32) for i in range(8)})
SEMAPHORES = (["dve", "act", "pe", "pool", "go"] + ["dm%d" % i for i in range(32)] + ["al%d" % t for t in range(RO)]
              + ["ar%d" % t for t in range(RO)] + ["at%d" % t for t in range(RO)] + ["ls%d" % t for t in range(RO)]
              + ["lt%d" % t for t in range(RO)])


def emit(g, T, ops):
    qs = {"dve": g.vector, "act": g.scalar, "pe": g.tensor, "pool": g, "sp": g.sync}
    seen, deps = {}, []
    for i, (q, fn, rd, wr, tok) in enumerate(ops):
        d = {}
        for acc, w in [(a, False) for a in rd] + [(a, True) for a in wr]:
            for (j, lo, hi, step, w2) in seen.get(acc[0], []):
                q2, tok2 = ops[j][0], ops[j][4]
                same = q2 == q and tok2 is None and tok is None
                bank = acc[0].startswith("ps") and not same
                if not bank and (hi <= acc[1] or lo >= acc[2] or not (w or w2)):
                    continue
                if same and CFG["comb"] and step == acc[3] and (lo - acc[1]) % step:
                    continue
                if same and (q == "pe" or (not (w2 and not w) and not CFG["waw"])):
                    continue
                key = q2 if tok2 is None else tok2[0]
                d[key] = max(d.get(key, -1), j)
        deps.append(d)
        for acc, w in [(a, False) for a in rd] + [(a, True) for a in wr]:
            seen.setdefault(acc[0], []).append((i, acc[1], acc[2], acc[3], w))
    got, need, known = {}, set(), []
    for i, d in enumerate(deps):
        mine = got.setdefault(ops[i][0], {})
        for key in sorted(d, key=lambda k: -d[k]):
            if mine.get(key, -1) >= d[key]:
                del d[key]
            else:
                mine[key] = d[key]
                need.add(d[key])
                if CFG["trans"]:
                    for k2, j2 in known[d[key]].items():
                        mine[k2] = max(mine.get(k2, -1), j2)
        known.append(dict(mine))
    last = {}
    for i, o in enumerate(ops):
        if o[4] is None:
            last[o[0]] = i
    need.update(last.values())
    cnt, val = {}, {}
    for i, (q, fn, rd, wr, tok) in enumerate(ops):
        if tok is not None:
            val[i] = tok
        elif i in need:
            cnt[q] = cnt.get(q, 0) + 1
            val[i] = (q, cnt[q])
    ends = {}
    for i, (q, fn, rd, wr, tok) in enumerate(ops):
        for key, j in deps[i].items():
            qs[q].wait_ge(T.sem[val[j][0]], val[j][1])
        if fn is not None:
            r = fn()
            if i in val and (tok is None or tok[0].startswith("dm")):
                r.then_inc(T.sem[val[i][0]], 1 if tok is None else 16)
        if i in val:
            ends[val[i][0]] = val[i][1]
    for s, v in ends.items():
        g.wait_ge(T.sem[s], v)


def rank_program(g, core, T, topo):
    r = T.rank_of(core)
    if r is None:
        return
    n = len(T.cores)
    prv, nxt = T.cores[(r - 1) % n], T.cores[(r + 1) % n]
    lowl, lowr = r < (r - 1) % n, r < (r + 1) % n
    dump = V if (lowl and lowr) else (V + RO * H if lowr else V + RO * H + V - H)
    ops, ndma = [], [0]

    def A(name, lo=0, hi=None, step=1):
        hi = T[name].shape[1] if hi is None else hi
        return (T[name][:, lo:hi:step] if step > 1 else T[name][:, lo:hi], [(name, lo, hi, step)])

    def X(win, off):
        return (win[0].indirect(off[0]), win[1], off[1])

    def sides(out, ins):
        rd = list(out[2]) if len(out) > 2 else []
        for a in ins:
            if isinstance(a, tuple):
                rd += a[1] + (a[2] if len(a) > 2 else [])
        return rd, out[1]

    def ap(a):
        return a[0] if isinstance(a, tuple) else a

    def rec(q, fn, out, ins, tok=None):
        rd, wr = sides(out, ins)
        ops.append((q, fn, rd, wr, tok))

    def cp(out, a):
        rec("dve", lambda: g.vector.tensor_copy(out[0], a[0]), out, [a])

    def ms(out, v):
        rec("dve", lambda: g.vector.memset(out[0], v), out, [])

    def tt(out, a, b, op):
        rec("dve", lambda: g.vector.tensor_tensor(out[0], a[0], b[0], op), out, [a, b])

    def ts(out, a, s1, op0, s2=None, op1=None):
        if op1 is None:
            rec("dve", lambda: g.vector.tensor_scalar(out[0], a[0], ap(s1), None, op0), out, [a, s1])
        else:
            rec("dve", lambda: g.vector.tensor_scalar(out[0], a[0], ap(s1), ap(s2), op0, op1), out, [a, s1, s2])

    def scan(out, a, b, ini, op0, op1):
        rec("dve", lambda: g.vector.tensor_tensor_scan(out[0], a[0], b[0], ap(ini), op0, op1), out, [a, b, ini])

    def act(out, a, fn, bias=None, scale=1.0):
        if bias is None:
            rec("act", lambda: g.scalar.activation(out[0], a[0], fn, scale=ap(scale)), out, [a, scale])
        else:
            rec("act", lambda: g.scalar.activation(out[0], a[0], fn, bias=bias[0], scale=scale), out, [a, bias])

    def mm(out, l, rh, start, stop):
        rec("pe", lambda: g.tensor.matmul(out[0], l[0], rh[0], start, stop), out, [l, rh])

    def iota(out, pat, base, cm, flt=True):
        if flt:
            rec("pool", lambda: g.iota(out[0], pat, base, cm, allow_small_or_imprecise_dtypes=True), out, [])
        else:
            rec("pool", lambda: g.iota(out[0], pat, base, cm), out, [])

    def dma(q, out, a):
        e = {"sp": g.sync, "act": g.scalar, "pool": g}[q]
        tok = ("dm%d" % ndma[0], 16)
        ndma[0] += 1
        rec(q, lambda: e.dma_start(out[0], a[0]), out, [a], tok)

    def hbm(a):
        return (a, [])

    def wrap(out, name, lo, hi, start=True, stop=True):
        for p in range(16):
            mm(out, A("ee", 128 * p, 128 * p + 128), A(name, lo + p, hi, 16), start and p == 0, stop and p == 15)

    def col(i):
        return A("cc", i, i + 1)

    dma("sp", A("b1s", 0, H), hbm(T.b1[:, 0:H]))
    dma("act", A("b2s", 0, H), hbm(T.b2[:, 0:H]))
    dma("sp", A("bw", 0, V), hbm(T.dist[:, :]))
    dma("sp", A("b1s", H, U), hbm(T.b1[:, H:U]))
    dma("sp", A("b2s", H, U), hbm(T.b2[:, H:U]))

    iota(A("pi", 0, 1), [[0, 1]], 0, 1, False)
    iota(A("ia"), [[16, 8], [0, 16]], 0, -1)
    iota(A("colp"), [[0, 12], [1, 16]], 0, 0)
    iota(A("ew"), [[16, 64]], 0, 0)
    iota(A("nege", 0, H), [[-1, H]], 0, 0)

    def fill(name, lo, hi, v):
        iota(A(name, lo, hi), [[0, hi - lo]], int(v), 0, SB[name][1] != I32)
    fill("zr", 0, 128, 0)
    fill("rm", 0, 480, CEN + YS)
    fill("tw", 0, RO * H, 0)
    if dump > V:
        fill("bw", V, V + RO * H, 0)
    fill("cw", 0, 648, -CEN - 1)
    for name, v in (("fre", -CEN - 1), ("z", 0), ("nz2", 0), ("nzb", 0), ("nsb", 1), ("fq", 0), ("m16", -16)):
        fill(name, 0, SB[name][0], v)
    fill("thr", 0, 16, 8)
    fill("thr", 16, 64, 0)
    for t in range(RO):
        fill("stp", 192 * t, 192 * t + 192, t + 1)
    fill("b1s", U, U + 8, 0)
    fill("b2s", U, U + 8, 0)
    iota(A("nege", H, U), [[-1, U - H]], -H, 0)
    iota(A("nege", U, U + 512), [[-1, 512]], 0, 0)
    if not lowl:
        dma("sp", A("tw", V, V + RO * H), A("tw", 0, RO * H))
    if lowr:
        dma("sp", A("tw", V - H, V), A("tw", 0, H))
    else:
        dma("sp", A("tw", 2 * V - H, 2 * V - H + RO * H), A("tw", 0, RO * H))
    for o in range(V + RO * H, dump, RO * H):
        dma("sp", A("bw", o, o + RO * H), A("bw", V, V + RO * H))
    ms(A("ee"), 0.0)
    ts(A("pi", 1, 2), A("pi", 0, 1), 15, ALU.bitwise_and)
    cp(col(0), A("pi", 1, 2))
    P = col(0)
    ts(A("k1"), A("ia"), -16.0, ALU.is_gt)
    ts(A("k2"), A("ia"), 0.0, ALU.is_le)
    tt(A("bm"), A("k1"), A("k2"), ALU.mult)
    ts(A("k1"), A("colp", 0, 128), P, ALU.is_equal)
    ts(A("k2"), A("colp", 0, 128), P, ALU.is_ge)
    ts(A("ta"), A("colp", 0, 16), P, ALU.is_le, 8192.0, ALU.mult)
    for k in range(3):
        ts(col(2 + k), P, float(k), ALU.is_equal)
    ms(col(20), CEN + YS)
    ms(col(21), 1.0)
    ts(A("ew"), A("ew"), P, ALU.add)
    for p in range(16):
        cp(A("ee", 128 * p + p, 128 * p + 128, 16), A("bm", p, 128, 16))
    for k in range(3):
        act(A("rr", 128 * k, 128 * k + 128), A("bm"), ACT.Copy, None, col(2 + k))
    ro = [0, 192, 336, 432]
    for q in range(4):
        for e in range(3):
            o = ro[q] + e * (64 - 16 * q)
            act(A("rm", o, o + 16), A("ta"), ACT.Identity, col(20))
    act(A("nr0"), A("rr", 0, 128), ACT.Copy, None, -1.0)
    act(A("e1f"), A("ee", 128, 256), ACT.Copy)
    act(A("e2f"), A("ee", 256, 384), ACT.Copy)
    act(A("ra"), A("ee", 0, 128), ACT.Copy, None, col(2))
    for p in range(16):
        act(A("sel", 8 * p, 8 * p + 8), A("bm", 0, 128, 16), ACT.Copy, None, A("k1", p, p + 1))
    cp(A("o1"), A("b1s", 0, H))
    cp(A("o2"), A("b2s", 0, H))
    ts(col(1), P, -LN, ALU.mult, LN * (15 - 144) - 54.0, ALU.add)
    tt(A("idn"), A("bm"), A("k1"), ALU.mult)
    tt(A("um"), A("bm"), A("k2"), ALU.mult)
    ts(A("k3"), A("bm"), -0.42, ALU.mult)
    tt(col(22), col(3), col(4), ALU.add)
    ts(A("i1"), A("ew"), 1.0, ALU.add)
    ts(A("lh"), A("nege", 0, H), -1.0, ALU.mult, -CEN, ALU.add)
    tt(A("mz"), A("k3"), A("idn"), ALU.add)
    ts(col(5), col(22), -CEN, ALU.mult)
    ts(A("dk"), A("zr"), col(2), ALU.subtract)
    tt(A("bu"), A("bm"), A("um"), ALU.subtract)
    ts(A("n64"), A("idn"), -64.0, ALU.mult)
    ts(A("gu"), A("ew", 0, 8), float(RP + 1), ALU.add)
    ts(A("xm"), A("colp"), P, ALU.is_equal, 8192 + CEN + YS, ALU.mult)
    ts(A("rst"), A("colp"), 0.0, ALU.is_gt, 32768.0, ALU.mult)
    ts(A("negm"), A("colp", 0, 64), P, ALU.is_equal, -1.0, ALU.add)
    ts(A("xm"), A("xm"), -8192.0, ALU.add)
    ts(A("rs64"), A("colp", 0, 64), 0.0, ALU.is_gt)
    for e in range(3):
        ms(col(10 + e), H * (e + 2) - 0.5)
    ts(A("dmp"), A("ew", 0, 12), dump + YS, ALU.add)
    ms(col(8), RL + H + 0.5)
    ms(col(9), 0.5)
    ms(col(13), 1.0 - U)
    ts(col(6), P, -1.0, ALU.mult, RL + 15.0, ALU.add)
    ms(col(7), 0.5 - CEN - YS)
    for t in range(1, 4):
        ts(col(15 + t), P, 128.0 * t + 1 - RL, ALU.add)
    ms(col(19), -float(U))
    ts(A("c16"), A("ew", 0, 8), -16.0, ALU.mult, 16.0 * (RP - TB), ALU.add)
    ts(A("c256"), A("ew", 0, 8), 256.0, ALU.mult, 256.0 * TB, ALU.add)

    D = A("bw", 0, V)
    parts, chunks = CFG["parts"], CFG["chunks"]
    npart = len(parts)
    e0 = [sum(parts[:i]) for i in range(npart + 1)]
    early, rep = e0[npart - 1], CFG["rep"]

    def look(t):
        def first(i):
            e = e0[i]
            for c in chunks[i]:
                act(A("s1", 16 * e, 16 * (e + c)), X(D, A("o1", e, e + c)), ACT.Copy)
                e += c
                if e > H - CFG["psadd"]:
                    o = 16 * (e - c - H + CFG["psadd"])
                    act(A("s2", o, o + 16 * c), X(D, A("o2", e - c, e)), ACT.Copy)
                    act(A("ps%d" % (6 + o // 512), o % 512, o % 512 + 16 * c), A("s2", o, o + 16 * c), ACT.Copy)
            for k in range(rep):
                act(A("ps%d" % (i % 2), k, rep * parts[i], rep), A("bw" if t == 0 else "de", e0[i], e0[i + 1]), ACT.Copy)

        def second(i):
            e = e0[i]
            for c in chunks[i]:
                o = 16 * (e - H + CFG["psadd"])
                two = X(D, A("o2", e, e + c)) if o < 0 else A("ps%d" % (6 + o // 512), o % 512, o % 512 + 16 * c)
                tt(A("sm", 16 * e, 16 * (e + c)), two, A("s1", 16 * e, 16 * (e + c)), ALU.add)
                e += c

        def compare(i):
            a, w = e0[i], parts[i]
            cnt = A("ps%d" % (2 + i % 2), 0, w)
            if t == RO - 1:
                mm(cnt, A("n64"), A("inv", a, a + w), True, False)
            st = 16 // rep
            for k in range(st):
                o = 16 * a + k * w * rep
                tt(A("cm", o, o + w * rep), A("sm", 16 * a + k, 16 * (a + w), st), A("ps%d" % (i % 2), 0, w * rep), ALU.is_lt)
                for j in range(rep):
                    kk = k + st * j
                    mm(cnt, A("ee", 128 * kk, 128 * kk + 128), A("cm", o + j, o + w * rep, rep),
                       k + j == 0 and t < RO - 1, k == st - 1 and j == rep - 1)

        def weigh(i):
            a, w = e0[i], parts[i]
            act(A("wx", a, a + w), A("ps%d" % (2 + i % 2), 0, w), ACT.Exp, col(1), 16 * LN)
            mm(A("ps4", 0, w), A("mz"), A("wx", a, a + w), True, True)

        def pick(i):
            a, w = e0[i], parts[i]
            o, c = (a, early + a) if i < npart - 1 else (2 * early, 2 * early + w)
            oh = A("oc", o, o + w)
            ts(oh, A("ps4", 0, w), 0.28 * math.exp(-54.0), ALU.is_gt)
            scan(A("oc", c, c + w), oh, A("dk", 0, w), 0.0 if i == 0 else A("oc", early + a - 1, early + a), ALU.add, ALU.add)
            if i == npart - 2:
                wrap(A("ps6", 0, early // 8), "oc", 0, 2 * early)
            if i == npart - 1:
                wrap(A("ps7", 0, w // 8), "oc", 2 * early, 2 * H)
            for b, pr in (("b1s", "p1"), ("b2s", "p2")):
                src = A(b, a, a + w) if t == 0 else X(A(b), A("lu", a // 16, (a + w) // 16))
                tt(A(pr, a, a + w), src, oh, ALU.mult)
            rt = A("ps5", 0, w)
            mm(rt, A("ra"), A("lh", a, a + w), True, False)
            mm(rt, A("e1f"), A("p1", a, a + w), False, False)
            mm(rt, A("e2f"), A("p2", a, a + w), False, True)

        def keep(i):
            act(A("rv", e0[i], e0[i + 1]), A("ps5", 0, parts[i]), ACT.Identity, col(5))

        def place(bank, a, b):
            m = b - a
            tt(A("ta", a, b), A(bank, 0, m), A("i1", a, b), ALU.mult)
            tt(A("tb", a, b), A("ta", a, b), A(bank, m, 2 * m), ALU.add)
            ts(A("pu", a, b), A("tb", a, b), float(RP), ALU.add)

        def put(a, b):
            cp(X(A("cw", 0, TB), A("pu", a, b)), A("rv", 16 * a, 16 * b))

        first(0)
        second(0)
        for i in range(npart):
            if i + 1 < npart:
                first(i + 1)
            if i > 0:
                pick(i - 1)
            compare(i)
            if i == npart - 1:
                keep(i - 1)
            weigh(i)
            if 0 < i < npart - 1:
                keep(i - 1)
            if i + 1 < npart:
                second(i + 1)
        ec, cut = early // 16, CFG["cut"]
        place("ps6", 0, ec)
        if cut:
            put(0, cut)
        pick(npart - 1)
        keep(npart - 1)
        put(cut, ec)
        place("ps7", ec, 16)
        put(ec, 16)

    def send(pairs, lsem):
        trs, rd, tot = [], [], 0
        for i, (src, core2, dst, sem) in enumerate(pairs):
            en = topo.engines(core, core2)
            k = len(en) // len(pairs)
            mask = sum(1 << e for e in en[i * k:(i + 1) * k])
            rid, pid = topo.addr(core2)[:2]
            trs.append((src[0], dst[0], sem, rid, pid, mask))
            rd += src[1]
            tot += k

        def fn():
            return g.remote_dma_fused([RemoteDMATransfer(dst_ids=[DstId(rid=x[3], pnc=x[4])], dma_engine_mask=x[5],
                                                         remote_sem=T.sem[x[2]], src=x[0], dst=x[1]) for x in trs],
                                      local_sem=T.sem[lsem])
        ops.append(("pool", fn, rd, [], (lsem, tot)))

    def lands(dst, sem, src_core, share):
        ops.append(("ext", None, [], dst[1], (sem, len(topo.engines(src_core, core)) // share)))

    for t in range(RO):
        par, sh = t % 2, V + H * t
        look(t)
        cp(A("th"), X(A("cw"), A("gu")))
        rows = [("ps3", 0), ("ps4", 0), ("ps5", 0), ("ps5", 96)]
        mm(A("ps2", 0, 192), A("idn"), A("xm"), True, False)
        for q in range(3):
            m = 192 if q == 0 else 144
            mm(A(rows[q][0], 0, m), A("idn"), A("rm", ro[q], ro[q] + m), True, False)
        for e in range(3):
            mm(A("ps2", 64 * e, 64 * e + 64), A("rr", 128 * e, 128 * e + 128), A("th", par, 128, 2), False, e == 2)
        ts(A("fr"), A("th"), -CEN - 1, ALU.is_equal)
        for q in range(4):
            w = 64 - 16 * q
            for e in range(3):
                o = rows[q][1] + e * w
                mm(A(rows[q][0], o, o + w), A("rr", 128 * e, 128 * e + 128), A("th", par + 32 * q, 128, 2), False, e == 2 and q != 2)
        scan(A("ys"), A("rst"), A("ps2", 0, 192), 0.0, ALU.min, ALU.max)
        Y = A("ys", 15, 192, 16)
        ts(A("yu"), Y, -YS, ALU.add)
        act(A("dg"), X(D, A("yu")), ACT.Copy)
        if dump > V and not lowr:
            act(A("ab"), Y, ACT.Abs, col(7))
        cnt = "ps0"
        mm(A(cnt, 0, 64), A("rr", 0, 128), A("fr", par, 128, 2), True, False)

        def hits(q):
            w = 64 - 16 * q
            for y in range(3):
                o = 480 * y + ro[q]
                ts(A("eq", o, o + 3 * w), A(rows[q][0], rows[q][1], rows[q][1] + 3 * w), A("ys", 64 * y + 16 * q + 15, 64 * y + 16 * q + 16), ALU.is_equal)
                for e in range(3):
                    mm(A(cnt, 16 * q, 64), A("bm"), A("eq", o + e * w, o + e * w + w), False, q == 3 and y == 2 and e == 2)

        def hits_s(y):
            for q, o, w in ((2, 0, 96), (3, 96, 48)):
                act(A("sq", 144 * y + o, 144 * y + o + w), A("ps5", o, o + w), ACT.Square, A("ys", 64 * y + 16 * q + 15, 64 * y + 16 * q + 16), -1.0)
            act(A("eqs", 144 * y, 144 * y + 144), A("sq", 144 * y, 144 * y + 144), ACT.Relu, col(21), -1.0)

        def count_s(y):
            for q, o, w in ((2, 0, 32), (3, 96, 16)):
                for e in range(3):
                    a = 144 * y + o + e * w
                    mm(A(cnt, 16 * q, 64), A("bm"), A("eqs", a, a + w), False, q == 3 and y == 2 and e == 2)
        if CFG["seq"]:
            hits_s(0)
        hits(0)
        base, src = "dg", Y
        if dump > V:
            if lowr:
                ts(A("mm"), Y, H + YS, ALU.is_lt, float(sh), ALU.mult)
            else:
                ts(A("mm"), A("ab"), V / 2.0 - H, ALU.is_ge, float(sh), ALU.mult)
            tt(A("mo"), A("mm"), Y, ALU.add)
            ts(A("mu"), A("mo"), -YS, ALU.add)
            base, src = "bs", A("mo")
        if CFG["seq"]:
            count_s(0)
            hits_s(1)
            hits_s(2)
        if dump > V:
            act(A("bs"), X(A("bw", 0, dump), A("mu")), ACT.Copy)
        tt(A("t1"), A("dg", 0, 64), A("dg", 64, 128), ALU.subtract)
        hits(1)
        if CFG["seq"]:
            count_s(1)
            count_s(2)
        else:
            hits(2)
        tt(A("t2"), A("t1"), A("dg", 128, 192), ALU.subtract)
        if not CFG["seq"]:
            hits(3)
        tt(A("d2"), A("t2"), A("nz2"), ALU.max)
        tt(A("pre"), src, A("dmp"), ALU.subtract)
        for e in range(3):
            act(A("dl", 64 * e, 64 * e + 64), A("d2"), ACT.Copy, None, -0.5 if e == 0 else 0.5)
        tt(A("mk"), A(cnt, 0, 64), A("negm"), ALU.is_equal)
        scan(A("sw"), A("rs64"), A("mk"), 0.0, ALU.mult, ALU.add)

        def places(pre, dm, mid, out):
            for e in range(3):
                tt(A(mid, 4 * e, 4 * e + 4), A(pre, 4 * e, 4 * e + 4), A("sw", 15, 64, 16), ALU.mult)
            tt(A(mid, 12, 24), A(mid, 0, 12), A(dm), ALU.add)
            ts(A(out), A(mid, 12, 24), -YS, ALU.add)

        def apply_d():
            tt(X(A("bw", 0, dump + 192), A("ou")), A(base), A("dl"), ALU.add)
            if t in (0, 3):
                tell()
            sl = A("bw", 0, H) if lowl else A("bw", sh, sh + H)
            sr = A("bw", V - H, V) if lowr else A("bw", sh + V - H, sh + V)
            send([(sl, prv, A("lr", H * t, H * t + H), "ar%d" % t), (sr, nxt, A("ll", H * t, H * t + H), "al%d" % t)], "ls%d" % t)
            act(A("ps1", 0, H), sl, ACT.Copy)
            act(A("ps1", H, 2 * H), sr, ACT.Copy)
            if t == RO - 1 and not CFG["hold"]:
                dma("sp", hbm(T.yd[:, H:V - H]), A("bw", H, V - H))

        def apply_t():
            if t == 3 and not lowr:
                for k in (1, 2):
                    wrap(A("ps7", 0, 16), "tw", 2 * V - H + H * k, 2 * V + H * k, k == 1, False)
            cp(X(A("tw", 0, dump + 192), A("ou")), A("stp", 192 * t, 192 * t + 192))
            if t in (0, 3, 4):
                o = V - H if lowr else sh + V - H
                wrap(A("ps7", 0, 16), "tw", o, o + H, lowr or t != 3)
            if lowl:
                wrap(A("ps6", 0, 64), "tw", 0, U)
            elif t == 0:
                wrap(A("ps5", 0, 16), "tw", sh, sh + H)
                wrap(A("ps6", 16, 64), "tw", H, U)
            else:
                wrap(A("ps6", 16, 64), "tw", H, U)

        def wrap_left():
            if not lowl and t > 0:
                wrap(A("ps5", 0, 16), "tw", sh, sh + H)

        def flags(name, o, a, b):
            for lo, hi, bank in ((max(a, 16), b, "ps6"), (a, min(b, 16), "ps6" if lowl else "ps5")):
                if lo < hi:
                    tt(A(name, o + lo - a, o + hi - a), A(bank, lo, hi), A("thr", lo, hi), ALU.is_ge)

        def tell():
            if t in (0, 3, 4):
                ts(A("ts", 16 * t, 16 * t + 16), A("ps7", 0, 16), {0: 8.0, 3: 24.0, 4: 72.0}[t], ALU.is_ge)
                send([(A("ts", 16 * t, 16 * t + 16), nxt, A("tl", 16 * t, 16 * t + 16), "at%d" % t)], "lt%d" % t)

        def forget():
            zv = A("z", par, 128, 2)
            tt(A("dm"), A("dl", 64, 128), A("sr"), ALU.mult)
            tt(zv, zv, A("dm"), ALU.add)
            ts(A("nzb", 128 * par + par, 128 * par + 128, 2), zv, 0.0, ALU.not_equal)
            cp(A("cw", TB, TB + 128), A("th"))
            act(A("cw", RP + 1, RP + 129), A("fre"), ACT.Copy)
            if t < RO - 1:
                act(A("nz2"), A("z", 1 - par, 128, 2), ACT.Copy, None, -2.0)
            else:
                dma("act", hbm(T.yz[:, :]), A("z"))

        def forget1():
            fc = A("ps0", 0, 128)
            mm(fc, A("nr0"), A("fr"), True, False)
            mm(fc, A("idn"), A("nsb", 128 * par, 128 * par + 128), False, False)
            mm(fc, A("bm"), A("nzb", 128 * par, 128 * par + 128), False, True)
            act(A("fs", 0, 128), A("ps0", 0, 128), ACT.Relu, col(21), -1.0)

        def forget2():
            scan(A("fs", 128, 256), A("fs", 0, 128), A("zr"), 0.0, ALU.add, ALU.add)
            wrap(A("ps4", 0, 16), "fs", 0, 256)

        def forget3(lo=0, hi=4):
            for k in range(lo, hi):
                if k == 0:
                    tt(A("g1"), A("ps4", 8, 16), A("c16"), ALU.add)
                elif k == 1:
                    tt(A("g2"), A("g1"), A("ps4", 0, 8), ALU.mult)
                elif k == 2:
                    tt(A("g3"), A("g2"), A("c256"), ALU.add)
                else:
                    ts(A("gu"), A("g3"), 1.0 / 256, ALU.mult)

        def add_shared():
            lands(A("ll", H * t, H * t + H), "al%d" % t, prv, 2)
            lands(A("lr", H * t, H * t + H), "ar%d" % t, nxt, 2)
            tt(A("bw", 0, H), A("ps1", 0, H), A("ll", H * t, H * t + H), ALU.add)
            if t == RO - 1:
                dma("sp", hbm(T.yd[:, 0:H]), A("bw", 0, H))
            tt(A("bw", V - H, V), A("ps1", H, 2 * H), A("lr", H * t, H * t + H), ALU.add)
            if t == RO - 1:
                dma("act", hbm(T.yd[:, V - H:V]), A("bw", V - H, V))

        places("pre", "dmp", "om", "ou")
        act(A("sr"), A(cnt, 0, 64), ACT.Relu, col(21), -1.0)
        act(A("nsb", 128 * par + par, 128 * par + 128, 2), A(cnt, 0, 64), ACT.Sign)
        if t in (0, 3):
            apply_t()
            apply_d()
        else:
            apply_d()
            apply_t()
            tell()
        told = A("tl", 16 * t, 16 * t + 16)
        if t == RO - 1:
            if CFG["hold"]:
                turn = [("turn", 0, 1, 1)]
                ops.append(("pool", lambda: g.sem_inc(T.sem["go"], 1), [], turn, ("go", 1)))
                dma("sp", hbm(T.yd[:, H:V - H]), (T["bw"][:, H:V - H], [("bw", H, V - H, 1)] + turn))

            def top(name, lo, hi, step=1):
                return (T[name][0:8, lo:hi:step] if step > 1 else T[name][0:8, lo:hi], [(name, lo, hi, step)])

            def unwrap(bank, a, b):
                m = 16 * (b - a)
                for p in range(16):
                    mm(top(bank, p, m, 16), A("sel", 8 * p, 8 * p + 8), A("fw", a, b), True, True)
                act(top("ft", 16 * a, 16 * b), top(bank, 0, m), ACT.Copy)
            forget()
            forget1()
            wrap_left()
            forget2()
            flags("fw", 0, 0, 64)
            unwrap("ps2", 16, 48)
            forget3()
            ts(A("tf"), X(A("cw"), A("gu")), CEN, ALU.add)
            unwrap("ps3", 48, 64)
            for e in range(3):
                dma("sp", hbm(T.yt[:, 128 * e:128 * e + 128]), (T["tf"][e:128:16, :], [("tf", 0, 128, 1)]))
            dma("sp", hbm(T.yf[:, H:U]), top("ft", H, U))
            add_shared()
            lands(told, "at%d" % t, prv, 1)
            tt(A("fw", 0, 16), A("fw", 0, 16), told, ALU.max)
            unwrap("ps5", 0, 16)
            dma("act", hbm(T.yf[:, 0:H]), top("ft", 0, H))
            break
        u = t + 1
        nc, c0, fo = (8 * u if u < 4 else 64), 8 * u, 68 * t
        pieces = [(c0, c0 + nc, 0)] if u < 4 else [(32, 64, 0), (0, 32, 32)]

        def pack(lo, hi, between=None):
            m = hi + 1 if hi == nc else hi
            mm(A("ps7", 0, m), A("um"), A("fq", fo + 1, fo + m + 1), True, False)
            mm(A("ps7", 0, m), A("bu"), A("fq", fo, fo + m), False, True)
            tt(A("f1", lo, hi), A("fq", fo + 1 + lo, fo + hi + 1), A("i1", lo, hi), ALU.mult)
            scan(A("sc", 0, m), A("ps7", 0, m), A("m16", 0, m), col(6), ALU.add, ALU.add)
            if u < 4:
                act(A("cn", 0, 1), A("sc", nc, nc + 1), ACT.Identity, col(15 + u))
                act(A("lw", RL + 1, RL + 1 + H), A("nege", H * u, H * u + H), ACT.Identity, A("cn", 0, 1))
            tt(A("of", lo, hi), A("sc", lo, hi), A("f1", lo, hi), ALU.add)
            cp(A("fu", lo, hi), A("of", lo, hi))
            if between:
                wrap_left()
                forget1()
            cp(X(A("lw"), A("fu", lo, hi)), A("nege", 128 * u + 16 * lo, 128 * u + 16 * hi))
        if u == 4:
            act(A("lw", RL + 1, RL + 1 + H), A("nege", 0, H), ACT.Identity, col(19), 0.0)
        forget()
        flags("fq", fo + 1, pieces[0][0], pieces[0][1])
        if t == 0:
            forget1()
            flags("fw", 0, 0, 64)
            forget2()
            forget3()
            lands(told, "at%d" % t, prv, 1)
            tt(A("fq", fo + 1, fo + 9), A("fq", fo + 1, fo + 9), A("tl", 8, 16), ALU.max)
            pack(0, nc)
        elif t == 3:
            pack(0, 32, True)
            flags("fq", fo + 33, 0, 32)
            lands(told, "at%d" % t, prv, 1)
            tt(A("fq", fo + 33, fo + 49), A("fq", fo + 33, fo + 49), told, ALU.max)
            pack(32, 64)
        else:
            pack(0, nc, True)
        ts(A("lh"), A("lw", RL + 1, RL + 1 + H), -1.0, ALU.mult, -CEN, ALU.add)
        wrap(A("ps7", 64, 80), "lh", 0, H)
        if t > 0:
            forget2()
            flags("fw", 0, 0, 64)
        if t in (0, 3):
            tt(A("fw", 0, 16), A("fw", 0, 16), told, ALU.max)
        if t == 3:
            add_shared()
        ts(A("lu"), A("ps7", 64, 80), 1.0 / 16, ALU.mult, CEN, ALU.add)
        cp(A("o1"), X(A("b1s"), A("lu")))
        if t > 0:
            forget3(0, 1)
        cp(A("o2"), X(A("b2s"), A("lu")))
        if t > 0:
            forget3(1, 2)
        for a, b, o in pieces:
            act(A("tq", a, b), A("of", o, o + b - a), ACT.Sign, col(8), -1.0)
        if u < 4:
            act(A("tq", 0, c0), A("fw", 0, c0), ACT.Sign, col(9), -1.0)
            act(A("cn", 1, 2), A("cn", 0, 1), ACT.Identity, col(9 + u), -1.0)
            act(A("tq", c0 + nc, 64), A("ew", c0 + nc, 64), ACT.Sign, A("cn", 1, 2), -1.0)
        else:
            act(A("inv"), A("lw", RL + 1, RL + 1 + H), ACT.Relu, col(13), -1.0)
        act(A("thr"), A("tq"), ACT.Relu, None, 16.0 * (u + 1) - 8)
        if t != 3:
            add_shared()
        if t > 0:
            forget3(2, 3)
        cp(A("de"), X(D, A("lu")))
        if t > 0:
            forget3(3, 4)
    emit(g, T, ops)
